import numpy as np
import ml_dtypes


def mxq(x, axis, fmt="e4m3"):
    dtype, down = {"e4m3": (ml_dtypes.float8_e4m3fn, 7), "e5m2": (ml_dtypes.float8_e5m2, 14)}[fmt]
    v = np.moveaxis(np.asarray(x, np.float32).astype(ml_dtypes.bfloat16).astype(np.float64), axis, -1)
    blocks = v.reshape(v.shape[:-1] + (-1, 32))
    amax = np.abs(blocks).max(-1, keepdims=True)
    byte = np.maximum(np.where(amax > 0, np.frexp(amax)[1] - 1 + 127, 0) - down, 1)
    scale = np.exp2(byte - 127.0)
    codes = (blocks / scale).astype(np.float32).astype(dtype).astype(np.float64)
    return np.moveaxis((codes * scale).reshape(v.shape), -1, axis)


WIDE = False


def mx_kscale(k):
    if not WIDE:
        return np.ones(k)
    levels = np.array([10, -10, 5, -5, 0])
    if k % 512:
        return np.exp2(np.random.permutation(np.resize(levels, k // 32))).repeat(32)
    a = np.empty((k // 512, 16))
    for p in range(k // 512):
        a[p, :8] = np.random.permutation(np.resize(levels, 8))
        for g in range(8):
            far = levels[np.abs(levels - a[p, g]) >= 10]
            a[p, g + 8] = far[np.random.randint(len(far))]
    return np.exp2(a.ravel()).repeat(32)


def f64(x):
    return np.asarray(x).astype(np.float64)


def striped(idx):
    return np.tile(idx.reshape(-1, 16).T, (8, 1)).astype(np.uint16)


def unstriped(offs):
    return offs[:16].T.reshape(-1).astype(np.int64)


E2M1 = np.array([0.0, 0.5, 1.0, 1.5, 2.0, 3.0, 4.0, 6.0, -0.0, -0.5, -1.0, -1.5, -2.0, -3.0, -4.0, -6.0])


def pack_weight(w, fmt):
    k, n = w.shape
    w = f64(np.asarray(w, np.float32).astype(ml_dtypes.bfloat16)).reshape(k // 32, 32, n)
    amax = np.abs(w).max(1)
    if fmt == "e4m3":
        byte = np.frexp(amax)[1] - 1 + 127 - 7
    else:
        mant, ex = np.frexp(amax / 6.0)
        byte = np.where(mant > 0.5, ex, ex - 1) + 127
    byte = np.clip(np.where(amax > 0, byte, 1), 1, 254)
    scaled = (w * np.exp2(127.0 - byte)[:, None, :]).reshape(k, n).astype(np.float32)
    by_word = np.ascontiguousarray(scaled.reshape(k // 512, 128, 4, n).transpose(0, 1, 3, 2))
    if fmt == "e4m3":
        words = by_word.astype(ml_dtypes.float8_e4m3fn).view(np.uint8)
    else:
        c = by_word.astype(ml_dtypes.float4_e2m1fn).view(np.uint8) & 0xF
        words = (c[..., 0::2] | (c[..., 1::2] << 4)).reshape(k // 512, 128, 2 * n)
    return np.ascontiguousarray(words), np.ascontiguousarray(byte.astype(np.uint8).reshape(k // 512, 16, n))


def unpack_weight(words, scales, fmt):
    g, _, n = scales.shape
    words = np.ascontiguousarray(words).reshape(g, 128, n, -1)
    if fmt == "e4m3":
        vals = words.view(ml_dtypes.float8_e4m3fn).astype(np.float64)
    else:
        nib = np.empty((g, 128, n, 4), np.uint8)
        nib[..., 0::2] = words & 0xF
        nib[..., 1::2] = words >> 4
        vals = E2M1[nib]
    vals = vals * np.repeat(np.exp2(scales.astype(np.float64) - 127.0), 8, axis=1)[..., None]
    return vals.transpose(0, 1, 3, 2).reshape(g * 512, n)


def gelu(v):
    return 0.5 * v * (1.0 + np.tanh(np.sqrt(2.0 / np.pi) * (v + 0.044715 * v**3)))


K, H, N, T, S, P = 1536, 1024, 512, 4096, 1024, 512

def setup_inputs():
    n = np.random.standard_normal
    s = mx_kscale(K)[:, None]
    u = mx_kscale(H)[:, None]
    tab_words, tab_scales = pack_weight(n((K, T)) * s, "e4m3")
    w1 = (n((K, H)) / np.sqrt(K) / s).astype(np.float32)
    gain = (1.5 * np.exp(0.3 * n(H))).astype(np.float32)
    va = (np.exp(0.3 * n(H)) * u[:, 0]).astype(np.float32)
    site = ((0.6 + 0.6 * n((H, P))) * u).astype(np.float32)
    bv = (0.8 * n(H) * u[:, 0]).astype(np.float32)
    wa_words, wa_scales = pack_weight(1.3 * n((H, N)) / np.sqrt(H) / u, "e2m1")
    wb = (0.8 * n((H, N)) / np.sqrt(H) / u).astype(np.float32)
    res = (0.8 * n((N, P))).astype(np.float32)
    offs = striped(np.random.permutation(T)[:S])
    pos1 = striped(np.random.permutation(S)[:P])
    pos2 = striped(np.random.permutation(S)[:P])
    return dict(tab_words=tab_words, tab_scales=tab_scales, offs=offs, pos1=pos1, pos2=pos2,
                w1=w1, gain=gain, va=va, site=site, bv=bv,
                wa_words=wa_words, wa_scales=wa_scales, wb=wb, res=res)

def reference(tab_words, tab_scales, offs, pos1, pos2, w1, gain, va, site, bv,
              wa_words, wa_scales, wb, res):
    v = unpack_weight(tab_words, tab_scales, "e4m3")[:, unstriped(offs)]
    h = f64(gain)[:, None] * (mxq(f64(w1), 0, "e4m3").T @ v)
    xa = np.tanh(h[:, unstriped(pos1)]) * f64(va)[:, None]
    xb = h[:, unstriped(pos2)] * f64(site) + f64(bv)[:, None]
    wa = unpack_weight(wa_words, wa_scales, "e2m1")
    ya = wa.T @ mxq(xa, 0, "e4m3")
    yb = mxq(f64(wb), 0, "e4m3").T @ mxq(xb, 0, "e4m3")
    return np.maximum(ya + f64(res), yb)

@@ -1,0 +1,241 @@
+from contextlib import ExitStack
+
+import concourse.mybir as mybir
+
+K, H, N, T, S, J = 1536, 1024, 512, 4096, 1024, 512
+FLOPS = 2 * K * H * S + 2 * 2 * H * N * J
+
+F32 = mybir.dt.float32
+BF16 = mybir.dt.bfloat16
+I32 = mybir.dt.int32
+U32 = mybir.dt.uint32
+U16 = mybir.dt.uint16
+U8 = mybir.dt.uint8
+FP8X4 = mybir.dt.float8_e4m3fn_x4
+FP4X4 = mybir.dt.float4_e2m1fn_x4
+ALU = mybir.AluOpType
+ACT = mybir.ActivationFunctionType
+
+P = 128
+PACK = 4
+KP = P * PACK
+BANK = 512
+
+
+def tile_list_wound_round_features_kernel(
+    tc, tab_words, tab_scales, offs, pos1, pos2, w1, gain, va, site, bv, wa_words, wa_scales, wb, res, out
+):
+    nc = tc.nc
+    passes = K // KP
+    blocks = H // KP
+    with ExitStack() as ctx:
+        lists = ctx.enter_context(tc.tile_pool(name="lists", bufs=1))
+        keep = ctx.enter_context(tc.tile_pool(name="keep", bufs=1))
+        ring = ctx.enter_context(tc.tile_pool(name="ring", bufs=1))
+        psum = ctx.enter_context(tc.psum_pool(name="psum", bufs=1))
+
+        offs_sb = lists.tile([P, S // 16], U16, name="offs_sb")
+        pos1_sb = lists.tile([P, J // 16], U16, name="pos1_sb")
+        pos2_sb = lists.tile([P, J // 16], U16, name="pos2_sb")
+
+        tab_sc = keep.tile([P, T], U8, name="tab_sc", align_bytes=64)
+        nc.vector.memset(tab_sc[:].bitcast(I32), 0)
+        def load_vec(src, name):
+            t = keep.tile([P, blocks, PACK], F32, name=name)
+            nc.gpsimd.dma_start(out=t[:], in_=src.rearrange("(b p t) -> p b t", p=P, t=PACK))
+            return t
+
+        gain_sb = load_vec(gain, "gain_sb")
+        va_sb = load_vec(va, "va_sb")
+        bv_sb = load_vec(bv, "bv_sb")
+        wa_sc = keep.tile([P, blocks, N], U8, name="wa_sc", align_bytes=64)
+        nc.gpsimd.memset(wa_sc[:].bitcast(I32), 0)
+        for q in range(4):
+            nc.gpsimd.dma_start(
+                out=wa_sc[32 * q : 32 * q + 4, :, :].bitcast(I32),
+                in_=wa_scales[:, 4 * q : 4 * q + 4, :].rearrange("a r c -> r a c").bitcast(I32),
+            )
+
+        def load_rows(src, name, tag, bufs):
+            t = ring.tile([P, PACK, BANK], F32, name=name, tag=tag, bufs=bufs, align_bytes=64)
+            nc.sync.dma_start(out=t[:], in_=src.rearrange("(p j) c -> p j c", j=PACK))
+            return t
+
+        def load_w1(a, b):
+            return load_rows(w1[KP * a : KP * (a + 1), KP * b : KP * (b + 1)], "w1_raw_%d_%d" % (a, b), "raw", 6)
+
+        tab_sb = []
+        w1_raw = {}
+        for a in range(passes):
+            t = keep.tile([P, T], I32, name="tab_%d" % a, align_bytes=64)
+            nc.sync.dma_start(out=t[:], in_=tab_words[a].rearrange("p t i -> p (t i)").bitcast(I32))
+            tab_sb.append(t)
+            if a == 0:
+                nc.sync.dma_start(offs_sb[:], offs)
+            w1_raw[a, 0] = load_w1(a, 0)
+            if a == 0:
+                for q in range(4):
+                    nc.sync.dma_start(
+                        out=tab_sc[32 * q : 32 * q + 4 * passes, :].bitcast(I32),
+                        in_=tab_scales[:, 4 * q : 4 * q + 4, :].bitcast(I32),
+                    )
+            if a == 1:
+                nc.sync.dma_start(pos1_sb[:], pos1)
+                nc.sync.dma_start(pos2_sb[:], pos2)
+        site_sb = [load_rows(site[0:KP, :], "site_0", "site", 2)]
+        for a in range(passes):
+            w1_raw[a, 1] = load_w1(a, 1)
+        site_sb.append(load_rows(site[KP : 2 * KP, :], "site_1", "site", 2))
+        wa_sb = keep.tile([P, blocks, 2 * N], U8, name="wa_sb", align_bytes=64)
+        nc.sync.dma_start(out=wa_sb[:].bitcast(I32), in_=wa_words.rearrange("a p c -> p a c").bitcast(I32))
+        wb_raw = [load_rows(wb[KP * b : KP * (b + 1), :], "wb_raw_%d" % b, "raw", 6) for b in range(blocks)]
+        res_sb = keep.tile([P, N // P, J], F32, name="res_sb")
+        nc.sync.dma_start(out=res_sb[:], in_=res.rearrange("(c p) j -> p c j", p=P))
+
+        v_sc = keep.tile([P, S], U8, name="v_sc", align_bytes=64)
+        v_words = [keep.tile([P, S], U32, name="v_words_%d" % a, align_bytes=64) for a in range(passes)]
+
+        def quantise(src, width, name, tag, bufs):
+            codes = ring.tile([P, width], U32, name=name + "_codes", tag=tag + "_codes", bufs=bufs, align_bytes=64)
+            scales = ring.tile([P, width], U8, name=name + "_sc", tag=tag + "_sc", bufs=bufs, align_bytes=64)
+            nc.vector.quantize_mx(out=codes[:].bitcast(FP8X4), scales=scales[:], in_=src)
+            return codes, scales
+
+        def round_w1(a, b, u, on_vector):
+            grouped = ring.tile([P, 2 * KP], BF16, name="w1_bf_%d_%d_%d" % (a, b, u), tag="w1_bf", bufs=4, align_bytes=64)
+            dst = grouped[:].rearrange("p (t m j) -> p m j t", t=2, j=PACK)
+            src = w1_raw[a, b][:].rearrange("p j (m t) -> p m j t", t=PACK)[:, :, :, 2 * u : 2 * u + 2]
+            if on_vector:
+                nc.vector.tensor_copy(out=dst, in_=src)
+            else:
+                nc.scalar.copy(out=dst, in_=src)
+            return grouped
+
+        def first_stage(b, h_psum):
+            for a in range(passes):
+                if b == 0:
+                    nc.vector.tensor_copy(out=v_words[a][:], in_=tab_sb[a][:].bitcast(U32).indirect(offs_sb[:]))
+                    if a == 0:
+                        nc.vector.tensor_copy(out=v_sc[:], in_=tab_sc[:].indirect(offs_sb[:]))
+                for u in range(2):
+                    grouped = round_w1(a, b, u, u == 0)
+                    codes, scales = quantise(grouped[:], 2 * P, "w1_%d_%d_%d" % (a, b, u), "w1", 8)
+                    for t2 in range(2):
+                        for half in range(2):
+                            cols = slice(BANK * half, BANK * (half + 1))
+                            nc.tensor.matmul_mx(
+                                out=h_psum[2 * (2 * u + t2) + half][:],
+                                lhsT=codes[:, P * t2 : P * (t2 + 1)].bitcast(FP8X4),
+                                lhsT_scale=scales[:, P * t2 : P * (t2 + 1)],
+                                rhs=v_words[a][:, cols].bitcast(FP8X4),
+                                rhs_scale=v_sc[4 * a : P, cols],
+                                start=(a == 0),
+                                stop=(a == passes - 1),
+                            )
+
+        def banks(name):
+            return [psum.tile([P, BANK], F32, name="%s_%d" % (name, i), tag="bank%d" % i) for i in range(8)]
+
+        def leave_psum(b, t, h_psum):
+            h = keep.tile([P, S], F32, name="h_%d_%d" % (b, t))
+            for half in range(2):
+                nc.scalar.activation(
+                    out=h[:, BANK * half : BANK * (half + 1)], in_=h_psum[2 * t + half][:],
+                    func=ACT.Copy, scale=gain_sb[:, b, t : t + 1],
+                )
+            return h
+
+        def pick_heel(b, t, h):
+            g = ring.tile([P, J], F32, name="heel_%d_%d" % (b, t), tag="picked", bufs=4)
+            nc.vector.tensor_copy(out=g[:], in_=h[:].indirect(pos1_sb[:]))
+            return g
+
+        def finish_heel(b, t, g, planes):
+            nc.scalar.activation(out=g[:], in_=g[:], func=ACT.Tanh)
+            nc.scalar.activation(out=planes[:, t, :], in_=g[:], func=ACT.Copy, scale=va_sb[:, b, t : t + 1])
+
+        def pick_sacral(b, t, h):
+            g = ring.tile([P, J], F32, name="sacral_%d_%d" % (b, t), tag="picked", bufs=4)
+            nc.vector.tensor_tensor(g[:], h[:].indirect(pos2_sb[:]), site_sb[b][:, t, :], ALU.mult)
+            return g
+
+        def finish_sacral(b, t, g, planes):
+            nc.scalar.activation(out=planes[:, t, :], in_=g[:], func=ACT.Identity, bias=bv_sb[:, b, t : t + 1])
+
+        def new_planes(name):
+            return ring.tile([P, PACK, J], BF16, name=name, tag="planes", bufs=2, align_bytes=64)
+
+        def weave(src, name, on_vector):
+            woven = ring.tile([P, BANK, PACK], BF16, name=name, tag="woven", bufs=2, align_bytes=64)
+            dst_ap = woven[:].rearrange("p (c i) t -> p c t i", i=4)
+            src_ap = src[:].rearrange("p t (c i) -> p c t i", i=4)
+            if on_vector:
+                nc.vector.tensor_copy(out=dst_ap, in_=src_ap)
+            else:
+                nc.scalar.copy(out=dst_ap, in_=src_ap)
+            return woven[:].rearrange("p c t -> p (c t)")
+
+        def heel_product(b, y):
+            for c in range(N // P):
+                nc.tensor.matmul_mx(
+                    out=y[c][:],
+                    lhsT=wa_sb[:, b, 2 * P * c : 2 * P * (c + 1)].bitcast(FP4X4),
+                    lhsT_scale=wa_sc[:, b, P * c : P * (c + 1)],
+                    rhs=xa[b][0][:].bitcast(FP8X4),
+                    rhs_scale=xa[b][1][:],
+                    start=(b == 0),
+                    stop=(b == blocks - 1),
+                )
+
+        def sacral_product(b, y):
+            for c in range(N // P):
+                nc.tensor.matmul_mx(
+                    out=y[4 + c][:],
+                    lhsT=wbq[b][0][:, P * c : P * (c + 1)].bitcast(FP8X4),
+                    lhsT_scale=wbq[b][1][:, P * c : P * (c + 1)],
+                    rhs=xb[b][0][:].bitcast(FP8X4),
+                    rhs_scale=xb[b][1][:],
+                    start=(b == 0),
+                    stop=(b == blocks - 1),
+                )
+
+        hp0 = banks("h0")
+        first_stage(0, hp0)
+        ga, gb, xa, xb = {}, {}, {}, {}
+        for t in range(PACK):
+            h = leave_psum(0, t, hp0)
+            ga[0, t] = pick_heel(0, t, h)
+            gb[0, t] = pick_sacral(0, t, h)
+        hp1 = banks("h1")
+        first_stage(1, hp1)
+        xa_planes, xb_planes = new_planes("xa_planes_0"), new_planes("xb_planes_0")
+        h1 = []
+        for t in range(PACK):
+            if t >= 2:
+                h1.append(leave_psum(1, 2 * (t - 2), hp1))
+                h1.append(leave_psum(1, 2 * (t - 2) + 1, hp1))
+            finish_heel(0, t, ga[0, t], xa_planes)
+            finish_sacral(0, t, gb[0, t], xb_planes)
+        for t in range(PACK):
+            ga[1, t] = pick_heel(1, t, h1[t])
+        xa[0] = quantise(weave(xa_planes, "xa_woven_0", False), J, "xa_0", "x", 4)
+        xb[0] = quantise(weave(xb_planes, "xb_woven_0", True), J, "xb_0", "x", 4)
+        xa_planes, xb_planes = new_planes("xa_planes_1"), new_planes("xb_planes_1")
+        for t in range(PACK):
+            finish_heel(1, t, ga[1, t], xa_planes)
+        wbq = [quantise(weave(wb_raw[b], "wb_woven_%d" % b, False), N, "wb_%d" % b, "wb", 2) for b in range(blocks)]
+        xa[1] = quantise(weave(xa_planes, "xa_woven_1", True), J, "xa_1", "x", 4)
+        y = banks("y")
+        heel_product(0, y)
+        sacral_product(0, y)
+        heel_product(1, y)
+        for t in range(PACK):
+            gb[1, t] = pick_sacral(1, t, h1[t])
+            finish_sacral(1, t, gb[1, t], xb_planes)
+        for c in range(N // P):
+            nc.vector.tensor_tensor(res_sb[:, c, :], y[c][:], res_sb[:, c, :], ALU.add)
+        xb[1] = quantise(weave(xb_planes, "xb_woven_1", True), J, "xb_1", "x", 4)
+        sacral_product(1, y)
+        for c in range(N // P):
+            nc.vector.tensor_tensor(res_sb[:, c, :], y[4 + c][:], res_sb[:, c, :], ALU.max)
+            nc.sync.dma_start(out=out[P * c : P * (c + 1), :], in_=res_sb[:, c, :])

@@ -38,23 +38,20 @@ def tile_list_wound_round_features_kernel(
         pos1_sb = lists.tile([P, J // 16], U16, name="pos1_sb")
         pos2_sb = lists.tile([P, J // 16], U16, name="pos2_sb")
 
-        tab_sc = keep.tile([P, T], U8, name="tab_sc", align_bytes=64)
-        nc.vector.memset(tab_sc[:].bitcast(I32), 0)
-        def load_vec(src, name):
-            t = keep.tile([P, blocks, PACK], F32, name=name)
-            nc.gpsimd.dma_start(out=t[:], in_=src.rearrange("(b p t) -> p b t", p=P, t=PACK))
-            return t
-
-        gain_sb = load_vec(gain, "gain_sb")
-        va_sb = load_vec(va, "va_sb")
-        bv_sb = load_vec(bv, "bv_sb")
-        wa_sc = keep.tile([P, blocks, N], U8, name="wa_sc", align_bytes=64)
-        nc.gpsimd.memset(wa_sc[:].bitcast(I32), 0)
+        tab_sc = ring.tile([P, T], U8, name="tab_sc", tag="scales_then_words", bufs=1, align_bytes=64)
+        nc.gpsimd.memset(tab_sc[:].bitcast(I32), 0)
         for q in range(4):
             nc.gpsimd.dma_start(
-                out=wa_sc[32 * q : 32 * q + 4, :, :].bitcast(I32),
-                in_=wa_scales[:, 4 * q : 4 * q + 4, :].rearrange("a r c -> r a c").bitcast(I32),
+                out=tab_sc[32 * q : 32 * q + 4 * passes, :].bitcast(I32),
+                in_=tab_scales[:, 4 * q : 4 * q + 4, :].bitcast(I32),
             )
+        def load_vec(src, name):
+            t = keep.tile([P, blocks, PACK], F32, name=name)
+            nc.sync.dma_start(out=t[:], in_=src.rearrange("(b p t) -> p b t", p=P, t=PACK))
+            return t
+
+        wa_sc = keep.tile([P, blocks, N], U8, name="wa_sc", align_bytes=64)
+        nc.vector.memset(wa_sc[:].bitcast(I32), 0)
 
         def load_rows(src, name, tag, bufs):
             t = ring.tile([P, PACK, BANK], F32, name=name, tag=tag, bufs=bufs, align_bytes=64)
@@ -62,38 +59,47 @@ def tile_list_wound_round_features_kernel(
             return t
 
         def load_w1(a, b):
-            return load_rows(w1[KP * a : KP * (a + 1), KP * b : KP * (b + 1)], "w1_raw_%d_%d" % (a, b), "raw", 6)
+            return load_rows(w1[KP * a : KP * (a + 1), KP * b : KP * (b + 1)], "w1_raw_%d_%d" % (a, b), "raw", 4)
 
-        tab_sb = []
-        w1_raw = {}
-        for a in range(passes):
+        def load_table(a):
             t = keep.tile([P, T], I32, name="tab_%d" % a, align_bytes=64)
             nc.sync.dma_start(out=t[:], in_=tab_words[a].rearrange("p t i -> p (t i)").bitcast(I32))
-            tab_sb.append(t)
-            if a == 0:
-                nc.sync.dma_start(offs_sb[:], offs)
-            w1_raw[a, 0] = load_w1(a, 0)
-            if a == 0:
-                for q in range(4):
-                    nc.sync.dma_start(
-                        out=tab_sc[32 * q : 32 * q + 4 * passes, :].bitcast(I32),
-                        in_=tab_scales[:, 4 * q : 4 * q + 4, :].bitcast(I32),
-                    )
-            if a == 1:
-                nc.sync.dma_start(pos1_sb[:], pos1)
-                nc.sync.dma_start(pos2_sb[:], pos2)
+            return t
+
+        w1_raw = {}
+        tab_sb = [load_table(0)]
+        nc.sync.dma_start(offs_sb[:], offs)
+        w1_raw[0, 0] = load_w1(0, 0)
+        tab_sb.append(load_table(1))
+        w1_raw[1, 0] = load_w1(1, 0)
+        nc.sync.dma_start(pos1_sb[:], pos1)
+        nc.sync.dma_start(pos2_sb[:], pos2)
+        gain_sb = load_vec(gain, "gain_sb")
+        tab_sb.append(load_table(2))
+        w1_raw[2, 0] = load_w1(2, 0)
         site_sb = [load_rows(site[0:KP, :], "site_0", "site", 2)]
         for a in range(passes):
             w1_raw[a, 1] = load_w1(a, 1)
+            if a == 0:
+                va_sb = load_vec(va, "va_sb")
+                bv_sb = load_vec(bv, "bv_sb")
         site_sb.append(load_rows(site[KP : 2 * KP, :], "site_1", "site", 2))
         wa_sb = keep.tile([P, blocks, 2 * N], U8, name="wa_sb", align_bytes=64)
         nc.sync.dma_start(out=wa_sb[:].bitcast(I32), in_=wa_words.rearrange("a p c -> p a c").bitcast(I32))
-        wb_raw = [load_rows(wb[KP * b : KP * (b + 1), :], "wb_raw_%d" % b, "raw", 6) for b in range(blocks)]
+        for q in range(4):
+            nc.sync.dma_start(
+                out=wa_sc[32 * q : 32 * q + 4, :, :].bitcast(I32),
+                in_=wa_scales[:, 4 * q : 4 * q + 4, :].rearrange("a r c -> r a c").bitcast(I32),
+            )
+        wb_raw = [load_rows(wb[KP * b : KP * (b + 1), :], "wb_raw_%d" % b, "raw", 4) for b in range(blocks)]
         res_sb = keep.tile([P, N // P, J], F32, name="res_sb")
         nc.sync.dma_start(out=res_sb[:], in_=res.rearrange("(c p) j -> p c j", p=P))
 
         v_sc = keep.tile([P, S], U8, name="v_sc", align_bytes=64)
-        v_words = [keep.tile([P, S], U32, name="v_words_%d" % a, align_bytes=64) for a in range(passes)]
+        v_words = [
+            ring.tile([P, S], U32, name="v_words_%d" % a, tag=("words_0", "scales_then_words", "words_2")[a], bufs=1, align_bytes=64)
+            for a in range(passes)
+        ]
 
         def quantise(src, width, name, tag, bufs):
             codes = ring.tile([P, width], U32, name=name + "_codes", tag=tag + "_codes", bufs=bufs, align_bytes=64)
@@ -102,7 +108,7 @@ def tile_list_wound_round_features_kernel(
             return codes, scales
 
         def round_w1(a, b, u, on_vector):
-            grouped = ring.tile([P, 2 * KP], BF16, name="w1_bf_%d_%d_%d" % (a, b, u), tag="w1_bf", bufs=4, align_bytes=64)
+            grouped = ring.tile([P, 2 * KP], BF16, name="w1_bf_%d_%d_%d" % (a, b, u), tag="w1_bf", bufs=6, align_bytes=64)
             dst = grouped[:].rearrange("p (t m j) -> p m j t", t=2, j=PACK)
             src = w1_raw[a, b][:].rearrange("p j (m t) -> p m j t", t=PACK)[:, :, :, 2 * u : 2 * u + 2]
             if on_vector:
@@ -146,7 +152,7 @@ def tile_list_wound_round_features_kernel(
             return h
 
         def pick_heel(b, t, h):
-            g = ring.tile([P, J], F32, name="heel_%d_%d" % (b, t), tag="picked", bufs=4)
+            g = ring.tile([P, J], F32, name="heel_%d_%d" % (b, t), tag="picked_%d" % b, bufs=(4, 4)[b])
             nc.vector.tensor_copy(out=g[:], in_=h[:].indirect(pos1_sb[:]))
             return g
 
@@ -155,7 +161,7 @@ def tile_list_wound_round_features_kernel(
             nc.scalar.activation(out=planes[:, t, :], in_=g[:], func=ACT.Copy, scale=va_sb[:, b, t : t + 1])
 
         def pick_sacral(b, t, h):
-            g = ring.tile([P, J], F32, name="sacral_%d_%d" % (b, t), tag="picked", bufs=4)
+            g = ring.tile([P, J], F32, name="sacral_%d_%d" % (b, t), tag="picked_%d" % b, bufs=(4, 4)[b])
             nc.vector.tensor_tensor(g[:], h[:].indirect(pos2_sb[:]), site_sb[b][:, t, :], ALU.mult)
             return g
 
@@ -163,7 +169,7 @@ def tile_list_wound_round_features_kernel(
             nc.scalar.activation(out=planes[:, t, :], in_=g[:], func=ACT.Identity, bias=bv_sb[:, b, t : t + 1])
 
         def new_planes(name):
-            return ring.tile([P, PACK, J], BF16, name=name, tag="planes", bufs=2, align_bytes=64)
+            return ring.tile([P, PACK, J], BF16, name=name, tag="planes", bufs=3, align_bytes=64)
 
         def weave(src, name, on_vector):
             woven = ring.tile([P, BANK, PACK], BF16, name=name, tag="woven", bufs=2, align_bytes=64)
@@ -218,7 +224,7 @@ def tile_list_wound_round_features_kernel(
             finish_sacral(0, t, gb[0, t], xb_planes)
         for t in range(PACK):
             ga[1, t] = pick_heel(1, t, h1[t])
-        xa[0] = quantise(weave(xa_planes, "xa_woven_0", False), J, "xa_0", "x", 4)
+        xa[0] = quantise(weave(xa_planes, "xa_woven_0", True), J, "xa_0", "x", 4)
         xb[0] = quantise(weave(xb_planes, "xb_woven_0", True), J, "xb_0", "x", 4)
         xa_planes, xb_planes = new_planes("xa_planes_1"), new_planes("xb_planes_1")
         for t in range(PACK):
@@ -234,7 +240,7 @@ def tile_list_wound_round_features_kernel(
             finish_sacral(1, t, gb[1, t], xb_planes)
         for c in range(N // P):
             nc.vector.tensor_tensor(res_sb[:, c, :], y[c][:], res_sb[:, c, :], ALU.add)
-        xb[1] = quantise(weave(xb_planes, "xb_woven_1", True), J, "xb_1", "x", 4)
+        xb[1] = quantise(weave(xb_planes, "xb_woven_1", False), J, "xb_1", "x", 4)
         sacral_product(1, y)
         for c in range(N // P):
             nc.vector.tensor_tensor(res_sb[:, c, :], y[4 + c][:], res_sb[:, c, :], ALU.max)

from contextlib import ExitStack

import concourse.mybir as mybir

K, H, N, T, S, J = 1536, 1024, 512, 4096, 1024, 512
FLOPS = 2 * K * H * S + 2 * 2 * H * N * J

F32 = mybir.dt.float32
BF16 = mybir.dt.bfloat16
I32 = mybir.dt.int32
U32 = mybir.dt.uint32
U16 = mybir.dt.uint16
U8 = mybir.dt.uint8
FP8X4 = mybir.dt.float8_e4m3fn_x4
FP4X4 = mybir.dt.float4_e2m1fn_x4
ALU = mybir.AluOpType
ACT = mybir.ActivationFunctionType

P = 128
PACK = 4
KP = P * PACK
BANK = 512


def tile_list_wound_round_features_kernel(
    tc, tab_words, tab_scales, offs, pos1, pos2, w1, gain, va, site, bv, wa_words, wa_scales, wb, res, out
):
    nc = tc.nc
    passes = K // KP
    blocks = H // KP
    with ExitStack() as ctx:
        lists = ctx.enter_context(tc.tile_pool(name="lists", bufs=1))
        keep = ctx.enter_context(tc.tile_pool(name="keep", bufs=1))
        ring = ctx.enter_context(tc.tile_pool(name="ring", bufs=1))
        psum = ctx.enter_context(tc.psum_pool(name="psum", bufs=1))

        offs_sb = lists.tile([P, S // 16], U16, name="offs_sb")
        pos1_sb = lists.tile([P, J // 16], U16, name="pos1_sb")
        pos2_sb = lists.tile([P, J // 16], U16, name="pos2_sb")

        tab_sc = ring.tile([P, T], U8, name="tab_sc", tag="scales_then_words", bufs=1, align_bytes=64)
        nc.gpsimd.memset(tab_sc[:].bitcast(I32), 0)
        for q in range(4):
            nc.gpsimd.dma_start(
                out=tab_sc[32 * q : 32 * q + 4 * passes, :].bitcast(I32),
                in_=tab_scales[:, 4 * q : 4 * q + 4, :].bitcast(I32),
            )
        def load_vec(src, name):
            t = keep.tile([P, blocks, PACK], F32, name=name)
            nc.sync.dma_start(out=t[:], in_=src.rearrange("(b p t) -> p b t", p=P, t=PACK))
            return t

        wa_sc = keep.tile([P, blocks, N], U8, name="wa_sc", align_bytes=64)
        nc.vector.memset(wa_sc[:].bitcast(I32), 0)

        def load_rows(src, name, tag, bufs):
            t = ring.tile([P, PACK, BANK], F32, name=name, tag=tag, bufs=bufs, align_bytes=64)
            nc.sync.dma_start(out=t[:], in_=src.rearrange("(p j) c -> p j c", j=PACK))
            return t

        def load_w1(a, b):
            return load_rows(w1[KP * a : KP * (a + 1), KP * b : KP * (b + 1)], "w1_raw_%d_%d" % (a, b), "raw", 4)

        def load_table(a):
            t = keep.tile([P, T], I32, name="tab_%d" % a, align_bytes=64)
            nc.sync.dma_start(out=t[:], in_=tab_words[a].rearrange("p t i -> p (t i)").bitcast(I32))
            return t

        w1_raw = {}
        tab_sb = [load_table(0)]
        nc.sync.dma_start(offs_sb[:], offs)
        w1_raw[0, 0] = load_w1(0, 0)
        tab_sb.append(load_table(1))
        w1_raw[1, 0] = load_w1(1, 0)
        nc.sync.dma_start(pos1_sb[:], pos1)
        nc.sync.dma_start(pos2_sb[:], pos2)
        gain_sb = load_vec(gain, "gain_sb")
        tab_sb.append(load_table(2))
        w1_raw[2, 0] = load_w1(2, 0)
        site_sb = [load_rows(site[0:KP, :], "site_0", "site", 2)]
        for a in range(passes):
            w1_raw[a, 1] = load_w1(a, 1)
            if a == 0:
                va_sb = load_vec(va, "va_sb")
                bv_sb = load_vec(bv, "bv_sb")
        site_sb.append(load_rows(site[KP : 2 * KP, :], "site_1", "site", 2))
        wa_sb = keep.tile([P, blocks, 2 * N], U8, name="wa_sb", align_bytes=64)
        nc.sync.dma_start(out=wa_sb[:].bitcast(I32), in_=wa_words.rearrange("a p c -> p a c").bitcast(I32))
        for q in range(4):
            nc.sync.dma_start(
                out=wa_sc[32 * q : 32 * q + 4, :, :].bitcast(I32),
                in_=wa_scales[:, 4 * q : 4 * q + 4, :].rearrange("a r c -> r a c").bitcast(I32),
            )
        wb_raw = [load_rows(wb[KP * b : KP * (b + 1), :], "wb_raw_%d" % b, "raw", 4) for b in range(blocks)]
        res_sb = keep.tile([P, N // P, J], F32, name="res_sb")
        nc.sync.dma_start(out=res_sb[:], in_=res.rearrange("(c p) j -> p c j", p=P))

        v_sc = keep.tile([P, S], U8, name="v_sc", align_bytes=64)
        v_words = [
            ring.tile([P, S], U32, name="v_words_%d" % a, tag=("words_0", "scales_then_words", "words_2")[a], bufs=1, align_bytes=64)
            for a in range(passes)
        ]

        def quantise(src, width, name, tag, bufs):
            codes = ring.tile([P, width], U32, name=name + "_codes", tag=tag + "_codes", bufs=bufs, align_bytes=64)
            scales = ring.tile([P, width], U8, name=name + "_sc", tag=tag + "_sc", bufs=bufs, align_bytes=64)
            nc.vector.quantize_mx(out=codes[:].bitcast(FP8X4), scales=scales[:], in_=src)
            return codes, scales

        def round_w1(a, b, u, on_vector):
            grouped = ring.tile([P, 2 * KP], BF16, name="w1_bf_%d_%d_%d" % (a, b, u), tag="w1_bf", bufs=6, align_bytes=64)
            dst = grouped[:].rearrange("p (t m j) -> p m j t", t=2, j=PACK)
            src = w1_raw[a, b][:].rearrange("p j (m t) -> p m j t", t=PACK)[:, :, :, 2 * u : 2 * u + 2]
            if on_vector:
                nc.vector.tensor_copy(out=dst, in_=src)
            else:
                nc.scalar.copy(out=dst, in_=src)
            return grouped

        def first_stage(b, h_psum):
            for a in range(passes):
                if b == 0:
                    nc.vector.tensor_copy(out=v_words[a][:], in_=tab_sb[a][:].bitcast(U32).indirect(offs_sb[:]))
                    if a == 0:
                        nc.vector.tensor_copy(out=v_sc[:], in_=tab_sc[:].indirect(offs_sb[:]))
                for u in range(2):
                    grouped = round_w1(a, b, u, u == 0)
                    codes, scales = quantise(grouped[:], 2 * P, "w1_%d_%d_%d" % (a, b, u), "w1", 8)
                    for t2 in range(2):
                        for half in range(2):
                            cols = slice(BANK * half, BANK * (half + 1))
                            nc.tensor.matmul_mx(
                                out=h_psum[2 * (2 * u + t2) + half][:],
                                lhsT=codes[:, P * t2 : P * (t2 + 1)].bitcast(FP8X4),
                                lhsT_scale=scales[:, P * t2 : P * (t2 + 1)],
                                rhs=v_words[a][:, cols].bitcast(FP8X4),
                                rhs_scale=v_sc[4 * a : P, cols],
                                start=(a == 0),
                                stop=(a == passes - 1),
                            )

        def banks(name):
            return [psum.tile([P, BANK], F32, name="%s_%d" % (name, i), tag="bank%d" % i) for i in range(8)]

        def leave_psum(b, t, h_psum):
            h = keep.tile([P, S], F32, name="h_%d_%d" % (b, t))
            for half in range(2):
                nc.scalar.activation(
                    out=h[:, BANK * half : BANK * (half + 1)], in_=h_psum[2 * t + half][:],
                    func=ACT.Copy, scale=gain_sb[:, b, t : t + 1],
                )
            return h

        def pick_heel(b, t, h):
            g = ring.tile([P, J], F32, name="heel_%d_%d" % (b, t), tag="picked_%d" % b, bufs=(4, 4)[b])
            nc.vector.tensor_copy(out=g[:], in_=h[:].indirect(pos1_sb[:]))
            return g

        def finish_heel(b, t, g, planes):
            nc.scalar.activation(out=g[:], in_=g[:], func=ACT.Tanh)
            nc.scalar.activation(out=planes[:, t, :], in_=g[:], func=ACT.Copy, scale=va_sb[:, b, t : t + 1])

        def pick_sacral(b, t, h):
            g = ring.tile([P, J], F32, name="sacral_%d_%d" % (b, t), tag="picked_%d" % b, bufs=(4, 4)[b])
            nc.vector.tensor_tensor(g[:], h[:].indirect(pos2_sb[:]), site_sb[b][:, t, :], ALU.mult)
            return g

        def finish_sacral(b, t, g, planes):
            nc.scalar.activation(out=planes[:, t, :], in_=g[:], func=ACT.Identity, bias=bv_sb[:, b, t : t + 1])

        def new_planes(name):
            return ring.tile([P, PACK, J], BF16, name=name, tag="planes", bufs=3, align_bytes=64)

        def weave(src, name, on_vector):
            woven = ring.tile([P, BANK, PACK], BF16, name=name, tag="woven", bufs=2, align_bytes=64)
            dst_ap = woven[:].rearrange("p (c i) t -> p c t i", i=4)
            src_ap = src[:].rearrange("p t (c i) -> p c t i", i=4)
            if on_vector:
                nc.vector.tensor_copy(out=dst_ap, in_=src_ap)
            else:
                nc.scalar.copy(out=dst_ap, in_=src_ap)
            return woven[:].rearrange("p c t -> p (c t)")

        def heel_product(b, y):
            for c in range(N // P):
                nc.tensor.matmul_mx(
                    out=y[c][:],
                    lhsT=wa_sb[:, b, 2 * P * c : 2 * P * (c + 1)].bitcast(FP4X4),
                    lhsT_scale=wa_sc[:, b, P * c : P * (c + 1)],
                    rhs=xa[b][0][:].bitcast(FP8X4),
                    rhs_scale=xa[b][1][:],
                    start=(b == 0),
                    stop=(b == blocks - 1),
                )

        def sacral_product(b, y):
            for c in range(N // P):
                nc.tensor.matmul_mx(
                    out=y[4 + c][:],
                    lhsT=wbq[b][0][:, P * c : P * (c + 1)].bitcast(FP8X4),
                    lhsT_scale=wbq[b][1][:, P * c : P * (c + 1)],
                    rhs=xb[b][0][:].bitcast(FP8X4),
                    rhs_scale=xb[b][1][:],
                    start=(b == 0),
                    stop=(b == blocks - 1),
                )

        hp0 = banks("h0")
        first_stage(0, hp0)
        ga, gb, xa, xb = {}, {}, {}, {}
        for t in range(PACK):
            h = leave_psum(0, t, hp0)
            ga[0, t] = pick_heel(0, t, h)
            gb[0, t] = pick_sacral(0, t, h)
        hp1 = banks("h1")
        first_stage(1, hp1)
        xa_planes, xb_planes = new_planes("xa_planes_0"), new_planes("xb_planes_0")
        h1 = []
        for t in range(PACK):
            if t >= 2:
                h1.append(leave_psum(1, 2 * (t - 2), hp1))
                h1.append(leave_psum(1, 2 * (t - 2) + 1, hp1))
            finish_heel(0, t, ga[0, t], xa_planes)
            finish_sacral(0, t, gb[0, t], xb_planes)
        for t in range(PACK):
            ga[1, t] = pick_heel(1, t, h1[t])
        xa[0] = quantise(weave(xa_planes, "xa_woven_0", True), J, "xa_0", "x", 4)
        xb[0] = quantise(weave(xb_planes, "xb_woven_0", True), J, "xb_0", "x", 4)
        xa_planes, xb_planes = new_planes("xa_planes_1"), new_planes("xb_planes_1")
        for t in range(PACK):
            finish_heel(1, t, ga[1, t], xa_planes)
        wbq = [quantise(weave(wb_raw[b], "wb_woven_%d" % b, False), N, "wb_%d" % b, "wb", 2) for b in range(blocks)]
        xa[1] = quantise(weave(xa_planes, "xa_woven_1", True), J, "xa_1", "x", 4)
        y = banks("y")
        heel_product(0, y)
        sacral_product(0, y)
        heel_product(1, y)
        for t in range(PACK):
            gb[1, t] = pick_sacral(1, t, h1[t])
            finish_sacral(1, t, gb[1, t], xb_planes)
        for c in range(N // P):
            nc.vector.tensor_tensor(res_sb[:, c, :], y[c][:], res_sb[:, c, :], ALU.add)
        xb[1] = quantise(weave(xb_planes, "xb_woven_1", False), J, "xb_1", "x", 4)
        sacral_product(1, y)
        for c in range(N // P):
            nc.vector.tensor_tensor(res_sb[:, c, :], y[4 + c][:], res_sb[:, c, :], ALU.max)
            nc.sync.dma_start(out=out[P * c : P * (c + 1), :], in_=res_sb[:, c, :])
